import numpy as np
import ml_dtypes


def mxq(x, axis, fmt="e4m3"):
    dtype, down = {"e4m3": (ml_dtypes.float8_e4m3fn, 7), "e5m2": (ml_dtypes.float8_e5m2, 14)}[fmt]
    v = np.moveaxis(np.asarray(x, np.float32).astype(ml_dtypes.bfloat16).astype(np.float64), axis, -1)
    blocks = v.reshape(v.shape[:-1] + (-1, 32))
    amax = np.abs(blocks).max(-1, keepdims=True)
    byte = np.maximum(np.where(amax > 0, np.frexp(amax)[1] - 1 + 127, 0) - down, 1)
    scale = np.exp2(byte - 127.0)
    codes = (blocks / scale).astype(np.float32).astype(dtype).astype(np.float64)
    return np.moveaxis((codes * scale).reshape(v.shape), -1, axis)


WIDE = False


def mx_kscale(k):
    if not WIDE:
        return np.ones(k)
    levels = np.array([10, -10, 5, -5, 0])
    if k % 512:
        return np.exp2(np.random.permutation(np.resize(levels, k // 32))).repeat(32)
    a = np.empty((k // 512, 16))
    for p in range(k // 512):
        a[p, :8] = np.random.permutation(np.resize(levels, 8))
        for g in range(8):
            far = levels[np.abs(levels - a[p, g]) >= 10]
            a[p, g + 8] = far[np.random.randint(len(far))]
    return np.exp2(a.ravel()).repeat(32)


def f64(x):
    return np.asarray(x).astype(np.float64)


def striped(idx):
    return np.tile(idx.reshape(-1, 16).T, (8, 1)).astype(np.uint16)


def unstriped(offs):
    return offs[:16].T.reshape(-1).astype(np.int64)


def pack_weight(w):
    k, n = w.shape
    w = f64(np.asarray(w, np.float32).astype(ml_dtypes.bfloat16)).reshape(k // 32, 32, n)
    amax = np.abs(w).max(1)
    byte = np.clip(np.where(amax > 0, np.frexp(amax)[1] - 1 + 127 - 7, 1), 1, 254)
    scaled = (w * np.exp2(127.0 - byte)[:, None, :]).reshape(k, n).astype(np.float32)
    words = np.ascontiguousarray(scaled.reshape(k // 512, 128, 4, n).transpose(0, 1, 3, 2)).astype(ml_dtypes.float8_e4m3fn).view(np.uint8)
    return words, np.ascontiguousarray(byte.astype(np.uint8).reshape(k // 512, 16, n))


def unpack_weight(words, scales):
    g, p, n, _ = words.shape
    vals = np.ascontiguousarray(words).view(ml_dtypes.float8_e4m3fn).astype(np.float64) * np.repeat(np.exp2(scales.astype(np.float64) - 127.0), 8, axis=1)[..., None]
    return vals.transpose(0, 1, 3, 2).reshape(g * 512, n)


def relu(v):
    return np.maximum(v, 0.0)


def sigmoid(v):
    return 1.0 / (1.0 + np.exp(-np.maximum(v, -700.0)))


K, T, S, D, H, V, Z, W = 512, 2048, 512, 2, 512, 256, 512, 2048
P = 2 ** 7


def setup_inputs():
    n = np.random.standard_normal
    s = mx_kscale(K)[:, None]
    packed_xT = pack_weight(n((K, T)) * s)
    packed_eT = pack_weight(n((K, W)) * s)
    return {
        "x_words": packed_xT[0],
        "x_scales": packed_xT[1],
        "w1": (n((K, H)) / np.sqrt(K) / s).astype(np.float32),
        "w2": (n((K, H)) / np.sqrt(K) / s).astype(np.float32),
        "e_words": packed_eT[0],
        "e_scales": packed_eT[1],
        "unit": (np.random.uniform(0.6, 1.4, (K, 1)) / np.sqrt(K) / s).astype(np.float32),
        "prior": (np.tile(np.random.uniform(0.05, 0.9, W), (P, 1))).astype(np.float32),
        "offs": striped(np.random.permutation(T)[:S]),
        "ent": striped(np.random.permutation(W)[:Z]),
        "cor": striped(np.random.permutation(V)),
    }


def reference(x_words, x_scales, w1, w2, e_words, e_scales, unit, prior, offs, ent, cor):
    xq = unpack_weight(x_words, x_scales)[:, unstriped(offs)]
    y = mxq(f64(w1), 0, "e4m3").T @ xq
    yw = mxq(f64(w2), 0, "e4m3").T @ xq
    yr = relu(y) - (0.5 * yw)
    ment = yr.reshape(len(yr), -1, D).max(axis=2)
    coh = ment * (sigmoid(ment[:, unstriped(cor)]))
    hid = f64(unit) * coh
    e_ent = unpack_weight(e_words, e_scales)[:, unstriped(ent)]
    sc = mxq(hid, 0, "e4m3").T @ e_ent
    lp = sc + np.log(f64(prior)[:1][:, unstriped(ent)])
    el = np.exp(2.0 * np.tanh(lp))
    lse = np.log(el.mean(axis=1, keepdims=True) + 0.05)
    return lp - lse

@@ -1,0 +1,209 @@
+import math
+from contextlib import ExitStack
+
+import concourse.mybir as mybir
+from concourse.masks import make_identity
+
+K, T, S, H, V, Z, W = 512, 2048, 512, 512, 256, 512, 2048
+FLOPS = 2 * K * H * S * 2 + 2 * H * V * Z
+
+F32 = mybir.dt.float32
+BF16 = mybir.dt.bfloat16
+I32 = mybir.dt.int32
+U32 = mybir.dt.uint32
+U16 = mybir.dt.uint16
+U8 = mybir.dt.uint8
+FP8X4 = mybir.dt.float8_e4m3fn_x4
+ALU = mybir.AluOpType
+ACT = mybir.ActivationFunctionType
+
+P = 128
+PACK = 4
+HALF = H // 2
+SPARE = 16
+TERMS = 64
+CENTRE = math.sqrt((math.exp(-2.0) + 0.05) * (math.exp(2.0) + 0.05))
+
+
+def tile_picked_yentity_nll_p_kernel(
+    tc, x_words, x_scales, w1, w2, e_words, e_scales, unit, prior, offs, ent, cor, out
+):
+    nc = tc.nc
+    with ExitStack() as ctx:
+        lists = ctx.enter_context(tc.tile_pool(name="lists", bufs=1))
+        sb = ctx.enter_context(tc.tile_pool(name="sb", bufs=1))
+        psum = ctx.enter_context(tc.psum_pool(name="psum", bufs=1))
+
+        def bank(b, name):
+            return psum.tile([P, 512], F32, name=name, tag="bank%d" % b)
+
+        offs_t = lists.tile([P, S // 16], U16, name="offs_t")
+        ent_t = lists.tile([P, Z // 16], U16, name="ent_t")
+        cor_t = lists.tile([P, V // 16], U16, name="cor_t")
+        x_table = sb.tile([P, T], U32, name="x_table")
+        e_table = sb.tile([P, W], U32, name="e_table")
+        x_bytes = sb.tile([P, T], U8, name="x_bytes")
+        e_bytes = sb.tile([P, W], U8, name="e_bytes")
+        prior_t = sb.tile([P, W], F32, name="prior_t")
+        unit_t = sb.tile([P, PACK], F32, name="unit_t")
+        raw = [[sb.tile([P, PACK, HALF], F32, name="raw%d_%d" % (a, h)) for h in range(2)] for a in range(2)]
+
+        def load_scales(queue, table, scales):
+            for r in range(4):
+                queue.dma_start(out=table[r:P:32, :].bitcast(I32), in_=scales[0, r:16:4, :].bitcast(I32))
+
+        def load_words(table, words):
+            nc.sync.dma_start(out=table[:].bitcast(I32), in_=words[0].rearrange("p n t -> p (n t)").bitcast(I32))
+
+        def load_weight(a, w):
+            rows = w.rearrange("(p j) c -> p j c", j=PACK)
+            for h in range(2):
+                nc.sync.dma_start(out=raw[a][h][:], in_=rows[:, :, h * HALF : (h + 1) * HALF])
+
+        ident = sb.tile([P, P], F32, name="ident")
+        make_identity(nc, ident[:])
+        nc.vector.memset(x_bytes[:].bitcast(I32), 0)
+        nc.vector.memset(e_bytes[:].bitcast(I32), 0)
+        nc.vector.memset(prior_t[0 : P - 1, :], 0.0)
+
+        nc.sync.dma_start(offs_t[:], offs)
+        nc.sync.dma_start(ent_t[:], ent)
+        nc.scalar.dma_start(out=prior_t[P - 1 : P, :], in_=prior[0:1, :])
+        load_words(x_table, x_words)
+        load_scales(nc.scalar, x_bytes, x_scales)
+        load_weight(0, w1)
+        nc.sync.dma_start(cor_t[:], cor)
+        load_weight(1, w2)
+        load_scales(nc.sync, e_bytes, e_scales)
+        load_words(e_table, e_words)
+        nc.gpsimd.dma_start(out=unit_t[:], in_=unit.rearrange("(p t) o -> p (t o)", t=PACK))
+
+        odd = sb.tile([P, TERMS // 2], F32, name="odd")
+        nc.gpsimd.iota(odd[:], pattern=[[-2, TERMS // 2]], base=TERMS - 1, channel_multiplier=0,
+                       allow_small_or_imprecise_dtypes=True)
+        half_odd = sb.tile([P, TERMS // 2], F32, name="half_odd")
+        nc.gpsimd.tensor_scalar(half_odd[:], odd[:], 0.5, 0.0, ALU.mult, ALU.add)
+        series = sb.tile([P, TERMS], F32, name="series")
+        nc.vector.memset(series[:], 0.0)
+        nc.vector.reciprocal(series[:, 0:TERMS:2], half_odd[:])
+        gates = [sb.tile([P, V + SPARE], F32, name="gate%d" % t) for t in range(PACK)]
+        for t in range(PACK):
+            nc.gpsimd.memset(gates[t][:, V:], 0.0)
+
+        prior_picked = sb.tile([P, Z], F32, name="prior_picked")
+        nc.vector.tensor_copy(prior_picked[:], prior_t[:].indirect(ent_t[:]))
+        turned = bank(4, "turned")
+        for c in range(Z // P):
+            nc.tensor.transpose(turned[:, c * P : (c + 1) * P], prior_picked[:, c * P : (c + 1) * P], ident[:])
+        log_col = sb.tile([P, Z // P], F32, name="log_col")
+        nc.scalar.activation(log_col[:], turned[:, P - 1 : Z : P], ACT.Ln)
+        spread = bank(5, "spread")
+        for c in range(Z // P):
+            nc.tensor.transpose(spread[:, c * P : (c + 1) * P], log_col[:, c : c + 1].to_broadcast([P, P]), ident[:])
+        log_prior = sb.tile([P, Z], F32, name="log_prior")
+        nc.scalar.copy(log_prior[:], spread[:])
+
+        x_codes = sb.tile([P, S], U32, name="x_codes", align_bytes=64)
+        x_plane = sb.tile([P, S], U8, name="x_plane", align_bytes=64)
+        nc.vector.tensor_copy(x_plane[:], x_bytes[:].indirect(offs_t[:]))
+        nc.vector.tensor_copy(x_codes[:], x_table[:].indirect(offs_t[:]))
+
+        w_codes, w_plane = [], []
+        for a in range(2):
+            grouped = sb.tile([P, PACK, P, PACK], BF16, name="grouped%d" % a, align_bytes=64)
+            for h in range(2):
+                dst = grouped[:, :, h * 64 : (h + 1) * 64, :].rearrange("p t m j -> p m t j")
+                src = raw[a][h][:].rearrange("p j (m t) -> p m t j", t=PACK)
+                if a == 0:
+                    nc.scalar.copy(dst, src)
+                else:
+                    nc.vector.tensor_copy(dst, src)
+            codes = sb.tile([P, H], U32, name="w_codes%d" % a, align_bytes=64)
+            plane = sb.tile([P, H], U8, name="w_plane%d" % a, align_bytes=64)
+            for t in range(PACK):
+                nc.vector.quantize_mx(
+                    out=codes[:, t * P : (t + 1) * P].bitcast(FP8X4),
+                    scales=plane[:, t * P : (t + 1) * P],
+                    in_=grouped[:, t, :, :].rearrange("p m j -> p (m j)"),
+                )
+            w_codes.append(codes)
+            w_plane.append(plane)
+
+        def product(acc, codes, plane, cols, rhs_codes, rhs_plane):
+            nc.tensor.matmul_mx(
+                out=acc[:],
+                lhsT=codes[:, cols].bitcast(FP8X4),
+                lhsT_scale=plane[:, cols],
+                rhs=rhs_codes[:].bitcast(FP8X4),
+                rhs_scale=rhs_plane[:],
+                start=True,
+                stop=True,
+            )
+
+        relus = []
+        for t in range(PACK):
+            y = bank(t, "y%d" % t)
+            product(y, w_codes[0], w_plane[0], slice(t * P, (t + 1) * P), x_codes, x_plane)
+            relu_y = sb.tile([P, S], F32, name="relu_y%d" % t)
+            nc.scalar.activation(relu_y[:], y[:], ACT.Relu)
+            relus.append(relu_y)
+
+        scaled = sb.tile([P, PACK, V], F32, name="scaled")
+        gated = sb.tile([P, PACK, V], F32, name="gated")
+        for t in range(PACK):
+            yw = bank(4 + t, "yw%d" % t)
+            product(yw, w_codes[1], w_plane[1], slice(t * P, (t + 1) * P), x_codes, x_plane)
+            yr = sb.tile([P, S], F32, name="yr%d" % t)
+            nc.vector.scalar_tensor_tensor(yr[:], yw[:], -0.5, relus[t][:], ALU.mult, ALU.add)
+            ment = sb.tile([P, V], F32, name="ment%d" % t)
+            nc.vector.tensor_tensor(ment[:], yr[:, 0:S:2], yr[:, 1:S:2], ALU.max)
+            nc.scalar.activation(gates[t][:, :V], ment[:], ACT.Tanh, scale=0.5)
+            nc.scalar.activation(gated[:, t, :], gates[t][:].indirect(cor_t[:]), ACT.Copy, bias=0.5, scale=0.5)
+            if t < 2:
+                nc.scalar.activation(scaled[:, t, :], ment[:], ACT.Copy, scale=unit_t[:, t : t + 1])
+            else:
+                nc.vector.tensor_scalar(scaled[:, t, :], ment[:], unit_t[:, t : t + 1], None, ALU.mult)
+
+        e_codes = sb.tile([P, Z], U32, name="e_codes", align_bytes=64)
+        e_plane = sb.tile([P, Z], U8, name="e_plane", align_bytes=64)
+        nc.vector.tensor_copy(e_plane[:], e_bytes[:].indirect(ent_t[:]))
+        nc.vector.tensor_copy(e_codes[:], e_table[:].indirect(ent_t[:]))
+
+        for b in range(V // P):
+            cols = slice(b * P, (b + 1) * P)
+            hid = sb.tile([P, P, PACK], BF16, name="hid%d" % b, align_bytes=64)
+            nc.vector.tensor_tensor(
+                hid[:].rearrange("p (c i) t -> p c t i", i=4),
+                scaled[:, :, cols].rearrange("p t (c i) -> p c t i", i=4),
+                gated[:, :, cols].rearrange("p t (c i) -> p c t i", i=4),
+                ALU.mult,
+            )
+            h_codes = sb.tile([P, P], U32, name="h_codes%d" % b, align_bytes=64)
+            h_plane = sb.tile([P, P], U8, name="h_plane%d" % b, align_bytes=64)
+            nc.vector.quantize_mx(
+                out=h_codes[:].bitcast(FP8X4), scales=h_plane[:], in_=hid[:].rearrange("p v t -> p (v t)")
+            )
+            sc = bank(b, "sc%d" % b)
+            product(sc, h_codes, h_plane, slice(0, P), e_codes, e_plane)
+            lp = sb.tile([P, Z], F32, name="lp%d" % b)
+            nc.vector.tensor_tensor(lp[:], sc[:], log_prior[:], ALU.add)
+            squashed = sb.tile([P, Z], F32, name="squashed%d" % b)
+            nc.scalar.activation(squashed[:], lp[:], ACT.Tanh)
+            el = sb.tile([P, Z], F32, name="el%d" % b)
+            total = sb.tile([P, 1], F32, name="total%d" % b)
+            nc.scalar.activation(el[:], squashed[:], ACT.Exp, scale=2.0, accum_out=total[:])
+            den = sb.tile([P, 1], F32, name="den%d" % b)
+            nc.vector.tensor_scalar(den[:], total[:], Z * (0.05 + CENTRE), None, ALU.add)
+            inv = sb.tile([P, 1], F32, name="inv%d" % b)
+            nc.vector.reciprocal(inv[:], den[:])
+            ratio = sb.tile([P, 1], F32, name="ratio%d" % b)
+            nc.vector.tensor_scalar(ratio[:], inv[:], -2.0 * Z * CENTRE, 1.0, ALU.mult, ALU.add)
+            horner = sb.tile([P, TERMS], F32, name="horner%d" % b)
+            nc.vector.tensor_tensor_scan(
+                horner[:], ratio[:].to_broadcast([P, TERMS]), series[:], 0.0, ALU.mult, ALU.add
+            )
+            result = sb.tile([P, Z], F32, name="result%d" % b)
+            nc.vector.tensor_scalar(
+                result[:], lp[:], horner[:, TERMS - 1 : TERMS], math.log(CENTRE), ALU.subtract, ALU.subtract
+            )
+            nc.sync.dma_start(out=out[cols, :], in_=result[:])

@@ -20,9 +20,9 @@ ACT = mybir.ActivationFunctionType
 P = 128
 PACK = 4
 HALF = H // 2
-SPARE = 16
 TERMS = 64
-CENTRE = math.sqrt((math.exp(-2.0) + 0.05) * (math.exp(2.0) + 0.05))
+SHIFT_ARG = 3.25
+CENTRE = math.exp(2.0 * SHIFT_ARG) / Z - 0.05
 
 
 def tile_picked_yentity_nll_p_kernel(
@@ -46,7 +46,8 @@ def tile_picked_yentity_nll_p_kernel(
         e_bytes = sb.tile([P, W], U8, name="e_bytes")
         prior_t = sb.tile([P, W], F32, name="prior_t")
         unit_t = sb.tile([P, PACK], F32, name="unit_t")
-        raw = [[sb.tile([P, PACK, HALF], F32, name="raw%d_%d" % (a, h)) for h in range(2)] for a in range(2)]
+        raw1 = sb.tile([P, PACK, H], F32, name="raw1")
+        raw2 = [sb.tile([P, PACK, HALF], F32, name="raw2_%d" % h, tag="raw2_%d" % h) for h in range(2)]
 
         def load_scales(queue, table, scales):
             for r in range(4):
@@ -55,28 +56,31 @@ def tile_picked_yentity_nll_p_kernel(
         def load_words(table, words):
             nc.sync.dma_start(out=table[:].bitcast(I32), in_=words[0].rearrange("p n t -> p (n t)").bitcast(I32))
 
-        def load_weight(a, w):
-            rows = w.rearrange("(p j) c -> p j c", j=PACK)
-            for h in range(2):
-                nc.sync.dma_start(out=raw[a][h][:], in_=rows[:, :, h * HALF : (h + 1) * HALF])
+        squashed = [sb.tile([P, Z + 1], F32, name="squashed%d" % b) for b in range(V // P)]
+        for b in range(V // P):
+            nc.vector.memset(squashed[b][:, Z:], SHIFT_ARG)
+        nc.gpsimd.memset(x_bytes[:].bitcast(I32), 0)
+        nc.gpsimd.memset(e_bytes[:].bitcast(I32), 0)
+        nc.vector.memset(prior_t[0 : P - 1, :], 0.0)
+        warm = sb.tile([P, 3], F32, name="warm")
+        nc.scalar.activation(warm[:, 0:1], squashed[0][:, Z:], ACT.Ln)
+
+        nc.sync.dma_start(ent_t[:], ent)
+        nc.sync.dma_start(out=prior_t[P - 1 : P, :], in_=prior[0:1, :])
+        nc.sync.dma_start(out=raw1[:], in_=w1.rearrange("(p j) c -> p j c", j=PACK))
+        nc.sync.dma_start(offs_t[:], offs)
+        load_scales(nc.sync, x_bytes, x_scales)
+        load_words(x_table, x_words)
+        load_scales(nc.sync, e_bytes, e_scales)
+        for h in range(2):
+            nc.sync.dma_start(
+                out=raw2[h][:], in_=w2.rearrange("(p j) c -> p j c", j=PACK)[:, :, h * HALF : (h + 1) * HALF]
+            )
+        nc.sync.dma_start(cor_t[:], cor)
+        load_words(e_table, e_words)
 
         ident = sb.tile([P, P], F32, name="ident")
         make_identity(nc, ident[:])
-        nc.vector.memset(x_bytes[:].bitcast(I32), 0)
-        nc.vector.memset(e_bytes[:].bitcast(I32), 0)
-        nc.vector.memset(prior_t[0 : P - 1, :], 0.0)
-
-        nc.sync.dma_start(offs_t[:], offs)
-        nc.sync.dma_start(ent_t[:], ent)
-        nc.scalar.dma_start(out=prior_t[P - 1 : P, :], in_=prior[0:1, :])
-        load_words(x_table, x_words)
-        load_scales(nc.scalar, x_bytes, x_scales)
-        load_weight(0, w1)
-        nc.sync.dma_start(cor_t[:], cor)
-        load_weight(1, w2)
-        load_scales(nc.sync, e_bytes, e_scales)
-        load_words(e_table, e_words)
-        nc.gpsimd.dma_start(out=unit_t[:], in_=unit.rearrange("(p t) o -> p (t o)", t=PACK))
 
         odd = sb.tile([P, TERMS // 2], F32, name="odd")
         nc.gpsimd.iota(odd[:], pattern=[[-2, TERMS // 2]], base=TERMS - 1, channel_multiplier=0,
@@ -84,14 +88,12 @@ def tile_picked_yentity_nll_p_kernel(
         half_odd = sb.tile([P, TERMS // 2], F32, name="half_odd")
         nc.gpsimd.tensor_scalar(half_odd[:], odd[:], 0.5, 0.0, ALU.mult, ALU.add)
         series = sb.tile([P, TERMS], F32, name="series")
-        nc.vector.memset(series[:], 0.0)
-        nc.vector.reciprocal(series[:, 0:TERMS:2], half_odd[:])
-        gates = [sb.tile([P, V + SPARE], F32, name="gate%d" % t) for t in range(PACK)]
-        for t in range(PACK):
-            nc.gpsimd.memset(gates[t][:, V:], 0.0)
+        nc.gpsimd.memset(series[:], 0.0)
+
+        nc.gpsimd.dma_start(out=unit_t[:], in_=unit.rearrange("(p t) o -> p (t o)", t=PACK))
 
         prior_picked = sb.tile([P, Z], F32, name="prior_picked")
-        nc.vector.tensor_copy(prior_picked[:], prior_t[:].indirect(ent_t[:]))
+        nc.scalar.activation(prior_picked[:], prior_t[:].indirect(ent_t[:]), ACT.Copy)
         turned = bank(4, "turned")
         for c in range(Z // P):
             nc.tensor.transpose(turned[:, c * P : (c + 1) * P], prior_picked[:, c * P : (c + 1) * P], ident[:])
@@ -100,34 +102,46 @@ def tile_picked_yentity_nll_p_kernel(
         spread = bank(5, "spread")
         for c in range(Z // P):
             nc.tensor.transpose(spread[:, c * P : (c + 1) * P], log_col[:, c : c + 1].to_broadcast([P, P]), ident[:])
-        log_prior = sb.tile([P, Z], F32, name="log_prior")
-        nc.scalar.copy(log_prior[:], spread[:])
 
-        x_codes = sb.tile([P, S], U32, name="x_codes", align_bytes=64)
-        x_plane = sb.tile([P, S], U8, name="x_plane", align_bytes=64)
-        nc.vector.tensor_copy(x_plane[:], x_bytes[:].indirect(offs_t[:]))
-        nc.vector.tensor_copy(x_codes[:], x_table[:].indirect(offs_t[:]))
+        nc.vector.reciprocal(series[:, 0:TERMS:2], half_odd[:])
 
-        w_codes, w_plane = [], []
-        for a in range(2):
-            grouped = sb.tile([P, PACK, P, PACK], BF16, name="grouped%d" % a, align_bytes=64)
+        def interleave(grouped, halves):
             for h in range(2):
                 dst = grouped[:, :, h * 64 : (h + 1) * 64, :].rearrange("p t m j -> p m t j")
-                src = raw[a][h][:].rearrange("p j (m t) -> p m t j", t=PACK)
-                if a == 0:
+                src = halves[h].rearrange("p j (m t) -> p m t j", t=PACK)
+                if h == 0:
                     nc.scalar.copy(dst, src)
                 else:
                     nc.vector.tensor_copy(dst, src)
-            codes = sb.tile([P, H], U32, name="w_codes%d" % a, align_bytes=64)
-            plane = sb.tile([P, H], U8, name="w_plane%d" % a, align_bytes=64)
+
+        def quantise(grouped, name):
+            codes = sb.tile([P, H], U32, name=name + "_codes", align_bytes=64)
+            plane = sb.tile([P, H], U8, name=name + "_plane", align_bytes=64)
             for t in range(PACK):
                 nc.vector.quantize_mx(
                     out=codes[:, t * P : (t + 1) * P].bitcast(FP8X4),
                     scales=plane[:, t * P : (t + 1) * P],
                     in_=grouped[:, t, :, :].rearrange("p m j -> p (m j)"),
                 )
-            w_codes.append(codes)
-            w_plane.append(plane)
+            return codes, plane
+
+        grouped1 = sb.tile([P, PACK, P, PACK], BF16, name="grouped1", align_bytes=64)
+        interleave(grouped1, [raw1[:, :, :HALF], raw1[:, :, HALF:]])
+        log_prior = sb.tile([P, Z], F32, name="log_prior")
+        nc.scalar.copy(log_prior[:], spread[:])
+        nc.scalar.activation(warm[:, 1:2], grouped1[:, 0, 0, 0:1], ACT.Sigmoid, bias=log_prior[:, 0:1])
+
+        x_codes = sb.tile([P, S], U32, name="x_codes", align_bytes=64)
+        x_plane = sb.tile([P, S], U8, name="x_plane", align_bytes=64)
+        e_plane = sb.tile([P, Z], U8, name="e_plane", align_bytes=64)
+        nc.vector.tensor_copy(x_plane[:], x_bytes[:].indirect(offs_t[:]))
+        w1_codes, w1_plane = quantise(grouped1, "w1")
+        nc.vector.tensor_copy(x_codes[:], x_table[:].indirect(offs_t[:]))
+        nc.vector.tensor_copy(e_plane[:], e_bytes[:].indirect(ent_t[:]))
+
+        grouped2 = sb.tile([P, PACK, P, PACK], BF16, name="grouped2", align_bytes=64)
+        interleave(grouped2, [raw2[0][:], raw2[1][:]])
+        w2_codes, w2_plane = quantise(grouped2, "w2")
 
         def product(acc, codes, plane, cols, rhs_codes, rhs_plane):
             nc.tensor.matmul_mx(
@@ -143,30 +157,41 @@ def tile_picked_yentity_nll_p_kernel(
         relus = []
         for t in range(PACK):
             y = bank(t, "y%d" % t)
-            product(y, w_codes[0], w_plane[0], slice(t * P, (t + 1) * P), x_codes, x_plane)
-            relu_y = sb.tile([P, S], F32, name="relu_y%d" % t)
+            product(y, w1_codes, w1_plane, slice(t * P, (t + 1) * P), x_codes, x_plane)
+            relu_y = sb.tile([P, S], F32, name="relu_y%d" % t, tag="raw2_0" if t == 0 else "relu_y%d" % t)
             nc.scalar.activation(relu_y[:], y[:], ACT.Relu)
             relus.append(relu_y)
 
         scaled = sb.tile([P, PACK, V], F32, name="scaled")
-        gated = sb.tile([P, PACK, V], F32, name="gated")
-        for t in range(PACK):
+        gated = [sb.tile([P, PACK, P], F32, name="gated%d" % b) for b in range(V // P)]
+
+        def difference(t):
             yw = bank(4 + t, "yw%d" % t)
-            product(yw, w_codes[1], w_plane[1], slice(t * P, (t + 1) * P), x_codes, x_plane)
-            yr = sb.tile([P, S], F32, name="yr%d" % t)
+            product(yw, w2_codes, w2_plane, slice(t * P, (t + 1) * P), x_codes, x_plane)
+            yr = sb.tile([P, S], F32, name="yr%d" % t, tag="yr%d" % t, align_bytes=64)
             nc.vector.scalar_tensor_tensor(yr[:], yw[:], -0.5, relus[t][:], ALU.mult, ALU.add)
+            return yr
+
+        def mention(t, yr):
             ment = sb.tile([P, V], F32, name="ment%d" % t)
             nc.vector.tensor_tensor(ment[:], yr[:, 0:S:2], yr[:, 1:S:2], ALU.max)
-            nc.scalar.activation(gates[t][:, :V], ment[:], ACT.Tanh, scale=0.5)
-            nc.scalar.activation(gated[:, t, :], gates[t][:].indirect(cor_t[:]), ACT.Copy, bias=0.5, scale=0.5)
-            if t < 2:
-                nc.scalar.activation(scaled[:, t, :], ment[:], ACT.Copy, scale=unit_t[:, t : t + 1])
-            else:
+            if t == PACK - 1:
                 nc.vector.tensor_scalar(scaled[:, t, :], ment[:], unit_t[:, t : t + 1], None, ALU.mult)
+            for b in range(V // P):
+                nc.scalar.activation(
+                    gated[b][:, t, :], ment[:].indirect(cor_t[:, b * P // 16 : (b + 1) * P // 16]), ACT.Sigmoid
+                )
+            if t < PACK - 1:
+                nc.scalar.activation(scaled[:, t, :], ment[:], ACT.Copy, scale=unit_t[:, t : t + 1])
 
-        e_codes = sb.tile([P, Z], U32, name="e_codes", align_bytes=64)
-        e_plane = sb.tile([P, Z], U8, name="e_plane", align_bytes=64)
-        nc.vector.tensor_copy(e_plane[:], e_bytes[:].indirect(ent_t[:]))
+        pending = difference(0)
+        for t in range(PACK):
+            following = difference(t + 1) if t + 1 < PACK else None
+            mention(t, pending)
+            pending = following
+        nc.scalar.activation(warm[:, 2:3], gated[1][:, PACK - 1, 0:1], ACT.Exp)
+
+        e_codes = sb.tile([P, Z], U32, name="e_codes", tag="yr%d" % (PACK - 1), align_bytes=64)
         nc.vector.tensor_copy(e_codes[:], e_table[:].indirect(ent_t[:]))
 
         for b in range(V // P):
@@ -175,7 +200,7 @@ def tile_picked_yentity_nll_p_kernel(
             nc.vector.tensor_tensor(
                 hid[:].rearrange("p (c i) t -> p c t i", i=4),
                 scaled[:, :, cols].rearrange("p t (c i) -> p c t i", i=4),
-                gated[:, :, cols].rearrange("p t (c i) -> p c t i", i=4),
+                gated[b][:].rearrange("p t (c i) -> p c t i", i=4),
                 ALU.mult,
             )
             h_codes = sb.tile([P, P], U32, name="h_codes%d" % b, align_bytes=64)
@@ -187,13 +212,10 @@ def tile_picked_yentity_nll_p_kernel(
             product(sc, h_codes, h_plane, slice(0, P), e_codes, e_plane)
             lp = sb.tile([P, Z], F32, name="lp%d" % b)
             nc.vector.tensor_tensor(lp[:], sc[:], log_prior[:], ALU.add)
-            squashed = sb.tile([P, Z], F32, name="squashed%d" % b)
-            nc.scalar.activation(squashed[:], lp[:], ACT.Tanh)
-            el = sb.tile([P, Z], F32, name="el%d" % b)
-            total = sb.tile([P, 1], F32, name="total%d" % b)
-            nc.scalar.activation(el[:], squashed[:], ACT.Exp, scale=2.0, accum_out=total[:])
+            nc.scalar.activation(squashed[b][:, :Z], lp[:], ACT.Tanh)
+            el = sb.tile([P, Z + 1], F32, name="el%d" % b)
             den = sb.tile([P, 1], F32, name="den%d" % b)
-            nc.vector.tensor_scalar(den[:], total[:], Z * (0.05 + CENTRE), None, ALU.add)
+            nc.scalar.activation(el[:], squashed[b][:], ACT.Exp, scale=2.0, accum_out=den[:])
             inv = sb.tile([P, 1], F32, name="inv%d" % b)
             nc.vector.reciprocal(inv[:], den[:])
             ratio = sb.tile([P, 1], F32, name="ratio%d" % b)

@@ -45,8 +45,8 @@ def tile_picked_yentity_nll_p_kernel(
         x_bytes = sb.tile([P, T], U8, name="x_bytes")
         e_bytes = sb.tile([P, W], U8, name="e_bytes")
         prior_t = sb.tile([P, W], F32, name="prior_t")
-        unit_t = sb.tile([P, PACK], F32, name="unit_t")
-        raw1 = sb.tile([P, PACK, H], F32, name="raw1")
+        unit_t = sb.tile([P, PACK], F32, name="unit_t", tag="unit", align_bytes=64)
+        raw1 = sb.tile([P, PACK, H], F32, name="raw1", tag="raw1")
         raw2 = [sb.tile([P, PACK, HALF], F32, name="raw2_%d" % h, tag="raw2_%d" % h) for h in range(2)]
 
         def load_scales(queue, table, scales):
@@ -97,11 +97,6 @@ def tile_picked_yentity_nll_p_kernel(
         turned = bank(4, "turned")
         for c in range(Z // P):
             nc.tensor.transpose(turned[:, c * P : (c + 1) * P], prior_picked[:, c * P : (c + 1) * P], ident[:])
-        log_col = sb.tile([P, Z // P], F32, name="log_col")
-        nc.scalar.activation(log_col[:], turned[:, P - 1 : Z : P], ACT.Ln)
-        spread = bank(5, "spread")
-        for c in range(Z // P):
-            nc.tensor.transpose(spread[:, c * P : (c + 1) * P], log_col[:, c : c + 1].to_broadcast([P, P]), ident[:])
 
         nc.vector.reciprocal(series[:, 0:TERMS:2], half_odd[:])
 
@@ -127,9 +122,14 @@ def tile_picked_yentity_nll_p_kernel(
 
         grouped1 = sb.tile([P, PACK, P, PACK], BF16, name="grouped1", align_bytes=64)
         interleave(grouped1, [raw1[:, :, :HALF], raw1[:, :, HALF:]])
+        log_col = sb.tile([P, Z // P], F32, name="log_col", tag="raw1")
+        nc.scalar.activation(log_col[:], turned[:, P - 1 : Z : P], ACT.Ln)
+        nc.scalar.activation(warm[:, 1:2], log_col[:, 0:1], ACT.Sigmoid)
+        spread = bank(5, "spread")
+        for c in range(Z // P):
+            nc.tensor.transpose(spread[:, c * P : (c + 1) * P], log_col[:, c : c + 1].to_broadcast([P, P]), ident[:])
         log_prior = sb.tile([P, Z], F32, name="log_prior")
         nc.scalar.copy(log_prior[:], spread[:])
-        nc.scalar.activation(warm[:, 1:2], grouped1[:, 0, 0, 0:1], ACT.Sigmoid, bias=log_prior[:, 0:1])
 
         x_codes = sb.tile([P, S], U32, name="x_codes", align_bytes=64)
         x_plane = sb.tile([P, S], U8, name="x_plane", align_bytes=64)
@@ -143,64 +143,69 @@ def tile_picked_yentity_nll_p_kernel(
         interleave(grouped2, [raw2[0][:], raw2[1][:]])
         w2_codes, w2_plane = quantise(grouped2, "w2")
 
-        def product(acc, codes, plane, cols, rhs_codes, rhs_plane):
+        def product(acc, lhs_codes, lhs_plane, rhs_codes, rhs_plane):
             nc.tensor.matmul_mx(
-                out=acc[:],
-                lhsT=codes[:, cols].bitcast(FP8X4),
-                lhsT_scale=plane[:, cols],
-                rhs=rhs_codes[:].bitcast(FP8X4),
-                rhs_scale=rhs_plane[:],
+                out=acc,
+                lhsT=lhs_codes.bitcast(FP8X4),
+                lhsT_scale=lhs_plane,
+                rhs=rhs_codes.bitcast(FP8X4),
+                rhs_scale=rhs_plane,
                 start=True,
                 stop=True,
             )
 
-        relus = []
+        relus = sb.tile([P, PACK, S], F32, name="relus", tag="raw2_0")
         for t in range(PACK):
             y = bank(t, "y%d" % t)
-            product(y, w1_codes, w1_plane, slice(t * P, (t + 1) * P), x_codes, x_plane)
-            relu_y = sb.tile([P, S], F32, name="relu_y%d" % t, tag="raw2_0" if t == 0 else "relu_y%d" % t)
-            nc.scalar.activation(relu_y[:], y[:], ACT.Relu)
-            relus.append(relu_y)
+            product(y[:], w1_codes[:, t * P : (t + 1) * P], w1_plane[:, t * P : (t + 1) * P], x_codes[:], x_plane[:])
+            nc.scalar.activation(relus[:, t, :], y[:], ACT.Relu)
 
         scaled = sb.tile([P, PACK, V], F32, name="scaled")
-        gated = [sb.tile([P, PACK, P], F32, name="gated%d" % b) for b in range(V // P)]
+        ments = [sb.tile([P, V], F32, name="ment%d" % t) for t in range(PACK)]
+
+        def gate(gated, t, b):
+            nc.scalar.activation(
+                gated[:, t, :], ments[t][:].indirect(cor_t[:, b * P // 16 : (b + 1) * P // 16]), ACT.Sigmoid
+            )
+
+        gated0 = sb.tile([P, PACK, P], F32, name="gated0")
 
         def difference(t):
             yw = bank(4 + t, "yw%d" % t)
-            product(yw, w2_codes, w2_plane, slice(t * P, (t + 1) * P), x_codes, x_plane)
+            product(yw[:], w2_codes[:, t * P : (t + 1) * P], w2_plane[:, t * P : (t + 1) * P], x_codes[:], x_plane[:])
             yr = sb.tile([P, S], F32, name="yr%d" % t, tag="yr%d" % t, align_bytes=64)
-            nc.vector.scalar_tensor_tensor(yr[:], yw[:], -0.5, relus[t][:], ALU.mult, ALU.add)
+            nc.vector.scalar_tensor_tensor(yr[:], yw[:], -0.5, relus[:, t, :], ALU.mult, ALU.add)
             return yr
 
         def mention(t, yr):
-            ment = sb.tile([P, V], F32, name="ment%d" % t)
-            nc.vector.tensor_tensor(ment[:], yr[:, 0:S:2], yr[:, 1:S:2], ALU.max)
-            if t == PACK - 1:
-                nc.vector.tensor_scalar(scaled[:, t, :], ment[:], unit_t[:, t : t + 1], None, ALU.mult)
-            for b in range(V // P):
-                nc.scalar.activation(
-                    gated[b][:, t, :], ment[:].indirect(cor_t[:, b * P // 16 : (b + 1) * P // 16]), ACT.Sigmoid
-                )
+            nc.vector.tensor_tensor(ments[t][:], yr[:, 0:S:2], yr[:, 1:S:2], ALU.max)
+            gate(gated0, t, 0)
             if t < PACK - 1:
-                nc.scalar.activation(scaled[:, t, :], ment[:], ACT.Copy, scale=unit_t[:, t : t + 1])
+                nc.scalar.activation(scaled[:, t, :], ments[t][:], ACT.Copy, scale=unit_t[:, t : t + 1])
+            else:
+                nc.vector.tensor_scalar(scaled[:, t, :], ments[t][:], unit_t[:, t : t + 1], None, ALU.mult)
 
         pending = difference(0)
         for t in range(PACK):
             following = difference(t + 1) if t + 1 < PACK else None
             mention(t, pending)
             pending = following
-        nc.scalar.activation(warm[:, 2:3], gated[1][:, PACK - 1, 0:1], ACT.Exp)
+        gated1 = sb.tile([P, PACK, P], F32, name="gated1", tag="yr%d" % (PACK - 1), align_bytes=64)
+        for t in range(PACK):
+            gate(gated1, t, 1)
+        nc.scalar.activation(warm[:, 2:3], gated1[:, PACK - 1, 0:1], ACT.Exp)
 
-        e_codes = sb.tile([P, Z], U32, name="e_codes", tag="yr%d" % (PACK - 1), align_bytes=64)
-        nc.vector.tensor_copy(e_codes[:], e_table[:].indirect(ent_t[:]))
+        def pick_entities(h, tag):
+            codes = sb.tile([P, HALF], U32, name="e_codes%d" % h, tag=tag, align_bytes=64)
+            nc.vector.tensor_copy(codes[:], e_table[:].indirect(ent_t[:, h * HALF // 16 : (h + 1) * HALF // 16]))
+            return codes
 
-        for b in range(V // P):
-            cols = slice(b * P, (b + 1) * P)
-            hid = sb.tile([P, P, PACK], BF16, name="hid%d" % b, align_bytes=64)
+        def hidden(b, gated):
+            hid = sb.tile([P, P, PACK], BF16, name="hid%d" % b, tag="hid%d" % b, align_bytes=64)
             nc.vector.tensor_tensor(
                 hid[:].rearrange("p (c i) t -> p c t i", i=4),
-                scaled[:, :, cols].rearrange("p t (c i) -> p c t i", i=4),
-                gated[b][:].rearrange("p t (c i) -> p c t i", i=4),
+                scaled[:, :, b * P : (b + 1) * P].rearrange("p t (c i) -> p c t i", i=4),
+                gated[:].rearrange("p t (c i) -> p c t i", i=4),
                 ALU.mult,
             )
             h_codes = sb.tile([P, P], U32, name="h_codes%d" % b, align_bytes=64)
@@ -208,11 +213,22 @@ def tile_picked_yentity_nll_p_kernel(
             nc.vector.quantize_mx(
                 out=h_codes[:].bitcast(FP8X4), scales=h_plane[:], in_=hid[:].rearrange("p v t -> p (v t)")
             )
-            sc = bank(b, "sc%d" % b)
-            product(sc, h_codes, h_plane, slice(0, P), e_codes, e_plane)
+            return h_codes, h_plane
+
+        e_codes = [pick_entities(0, "unit")]
+        hidden_mx = [hidden(0, gated0)]
+        e_codes.append(pick_entities(1, "hid0"))
+        hidden_mx.append(hidden(1, gated1))
+
+        for b in range(V // P):
+            h_codes, h_plane = hidden_mx[b]
             lp = sb.tile([P, Z], F32, name="lp%d" % b)
-            nc.vector.tensor_tensor(lp[:], sc[:], log_prior[:], ALU.add)
-            nc.scalar.activation(squashed[b][:, :Z], lp[:], ACT.Tanh)
+            for h in range(2):
+                cols = slice(h * HALF, (h + 1) * HALF)
+                sc = bank(2 * b + h, "sc%d_%d" % (b, h))
+                product(sc[:, :HALF], h_codes[:], h_plane[:], e_codes[h][:], e_plane[:, cols])
+                nc.vector.tensor_tensor(lp[:, cols], sc[:, :HALF], log_prior[:, cols], ALU.add)
+                nc.scalar.activation(squashed[b][:, cols], lp[:, cols], ACT.Tanh)
             el = sb.tile([P, Z + 1], F32, name="el%d" % b)
             den = sb.tile([P, 1], F32, name="den%d" % b)
             nc.scalar.activation(el[:], squashed[b][:], ACT.Exp, scale=2.0, accum_out=den[:])
@@ -225,7 +241,10 @@ def tile_picked_yentity_nll_p_kernel(
                 horner[:], ratio[:].to_broadcast([P, TERMS]), series[:], 0.0, ALU.mult, ALU.add
             )
             result = sb.tile([P, Z], F32, name="result%d" % b)
-            nc.vector.tensor_scalar(
-                result[:], lp[:], horner[:, TERMS - 1 : TERMS], math.log(CENTRE), ALU.subtract, ALU.subtract
-            )
-            nc.sync.dma_start(out=out[cols, :], in_=result[:])
+            for h in range(2):
+                cols = slice(h * HALF, (h + 1) * HALF)
+                nc.vector.tensor_scalar(
+                    result[:, cols], lp[:, cols], horner[:, TERMS - 1 : TERMS], math.log(CENTRE),
+                    ALU.subtract, ALU.subtract,
+                )
+                nc.sync.dma_start(out=out[b * P : (b + 1) * P, cols], in_=result[:, cols])

@@ -19,7 +19,13 @@ ACT = mybir.ActivationFunctionType
 
 P = 128
 PACK = 4
-HALF = H // 2
+BANK = 512
+GROUP = 16
+SCALE_ROWS = K // 32
+W_HALF = H // 2
+Z_HALF = Z // 2
+BLOCKS = V // P
+
 TERMS = 64
 SHIFT_ARG = 3.25
 CENTRE = math.exp(2.0 * SHIFT_ARG) / Z - 0.05
@@ -34,33 +40,35 @@ def tile_picked_yentity_nll_p_kernel(
         sb = ctx.enter_context(tc.tile_pool(name="sb", bufs=1))
         psum = ctx.enter_context(tc.psum_pool(name="psum", bufs=1))
 
-        def bank(b, name):
-            return psum.tile([P, 512], F32, name=name, tag="bank%d" % b)
+        def bank(number, name):
+            return psum.tile([P, BANK], F32, name=name, tag="bank%d" % number)
 
-        offs_t = lists.tile([P, S // 16], U16, name="offs_t")
-        ent_t = lists.tile([P, Z // 16], U16, name="ent_t")
-        cor_t = lists.tile([P, V // 16], U16, name="cor_t")
+        offs_t = lists.tile([P, S // GROUP], U16, name="offs_t")
+        ent_t = lists.tile([P, Z // GROUP], U16, name="ent_t")
+        cor_t = lists.tile([P, V // GROUP], U16, name="cor_t")
         x_table = sb.tile([P, T], U32, name="x_table")
         e_table = sb.tile([P, W], U32, name="e_table")
         x_bytes = sb.tile([P, T], U8, name="x_bytes")
         e_bytes = sb.tile([P, W], U8, name="e_bytes")
         prior_t = sb.tile([P, W], F32, name="prior_t")
-        unit_t = sb.tile([P, PACK], F32, name="unit_t", tag="unit", align_bytes=64)
+        unit_t = sb.tile([P, PACK], F32, name="unit_t")
         raw1 = sb.tile([P, PACK, H], F32, name="raw1", tag="raw1")
-        raw2 = [sb.tile([P, PACK, HALF], F32, name="raw2_%d" % h, tag="raw2_%d" % h) for h in range(2)]
+        raw2 = [
+            sb.tile([P, PACK, W_HALF], F32, name="raw2_%d" % h, tag="raw2_%d" % h, align_bytes=64) for h in range(2)
+        ]
 
-        def load_scales(queue, table, scales):
+        def load_scales(table, scales):
             for r in range(4):
-                queue.dma_start(out=table[r:P:32, :].bitcast(I32), in_=scales[0, r:16:4, :].bitcast(I32))
+                nc.sync.dma_start(out=table[r:P:32, :].bitcast(I32), in_=scales[0, r:SCALE_ROWS:4, :].bitcast(I32))
 
         def load_words(table, words):
             nc.sync.dma_start(out=table[:].bitcast(I32), in_=words[0].rearrange("p n t -> p (n t)").bitcast(I32))
 
-        squashed = [sb.tile([P, Z + 1], F32, name="squashed%d" % b) for b in range(V // P)]
-        for b in range(V // P):
+        squashed = [sb.tile([P, Z + 1], F32, name="squashed%d" % b) for b in range(BLOCKS)]
+        for b in range(BLOCKS):
             nc.vector.memset(squashed[b][:, Z:], SHIFT_ARG)
-        nc.gpsimd.memset(x_bytes[:].bitcast(I32), 0)
-        nc.gpsimd.memset(e_bytes[:].bitcast(I32), 0)
+        nc.vector.memset(x_bytes[:].bitcast(I32), 0)
+        nc.vector.memset(e_bytes[:].bitcast(I32), 0)
         nc.vector.memset(prior_t[0 : P - 1, :], 0.0)
         warm = sb.tile([P, 3], F32, name="warm")
         nc.scalar.activation(warm[:, 0:1], squashed[0][:, Z:], ACT.Ln)
@@ -69,22 +77,27 @@ def tile_picked_yentity_nll_p_kernel(
         nc.sync.dma_start(out=prior_t[P - 1 : P, :], in_=prior[0:1, :])
         nc.sync.dma_start(out=raw1[:], in_=w1.rearrange("(p j) c -> p j c", j=PACK))
         nc.sync.dma_start(offs_t[:], offs)
-        load_scales(nc.sync, x_bytes, x_scales)
+        load_scales(x_bytes, x_scales)
         load_words(x_table, x_words)
-        load_scales(nc.sync, e_bytes, e_scales)
+        load_scales(e_bytes, e_scales)
         for h in range(2):
             nc.sync.dma_start(
-                out=raw2[h][:], in_=w2.rearrange("(p j) c -> p j c", j=PACK)[:, :, h * HALF : (h + 1) * HALF]
+                out=raw2[h][:], in_=w2.rearrange("(p j) c -> p j c", j=PACK)[:, :, h * W_HALF : (h + 1) * W_HALF]
             )
-        nc.sync.dma_start(cor_t[:], cor)
         load_words(e_table, e_words)
+        nc.sync.dma_start(cor_t[:], cor)
 
         ident = sb.tile([P, P], F32, name="ident")
         make_identity(nc, ident[:])
 
         odd = sb.tile([P, TERMS // 2], F32, name="odd")
-        nc.gpsimd.iota(odd[:], pattern=[[-2, TERMS // 2]], base=TERMS - 1, channel_multiplier=0,
-                       allow_small_or_imprecise_dtypes=True)
+        nc.gpsimd.iota(
+            odd[:],
+            pattern=[[-2, TERMS // 2]],
+            base=TERMS - 1,
+            channel_multiplier=0,
+            allow_small_or_imprecise_dtypes=True,
+        )
         half_odd = sb.tile([P, TERMS // 2], F32, name="half_odd")
         nc.gpsimd.tensor_scalar(half_odd[:], odd[:], 0.5, 0.0, ALU.mult, ALU.add)
         series = sb.tile([P, TERMS], F32, name="series")
@@ -101,8 +114,9 @@ def tile_picked_yentity_nll_p_kernel(
         nc.vector.reciprocal(series[:, 0:TERMS:2], half_odd[:])
 
         def interleave(grouped, halves):
+            span = W_HALF // PACK
             for h in range(2):
-                dst = grouped[:, :, h * 64 : (h + 1) * 64, :].rearrange("p t m j -> p m t j")
+                dst = grouped[:, :, h * span : (h + 1) * span, :].rearrange("p t m j -> p m t j")
                 src = halves[h].rearrange("p j (m t) -> p m t j", t=PACK)
                 if h == 0:
                     nc.scalar.copy(dst, src)
@@ -121,7 +135,8 @@ def tile_picked_yentity_nll_p_kernel(
             return codes, plane
 
         grouped1 = sb.tile([P, PACK, P, PACK], BF16, name="grouped1", align_bytes=64)
-        interleave(grouped1, [raw1[:, :, :HALF], raw1[:, :, HALF:]])
+        interleave(grouped1, [raw1[:, :, :W_HALF], raw1[:, :, W_HALF:]])
+
         log_col = sb.tile([P, Z // P], F32, name="log_col", tag="raw1")
         nc.scalar.activation(log_col[:], turned[:, P - 1 : Z : P], ACT.Ln)
         nc.scalar.activation(warm[:, 1:2], log_col[:, 0:1], ACT.Sigmoid)
@@ -154,81 +169,63 @@ def tile_picked_yentity_nll_p_kernel(
                 stop=True,
             )
 
-        relus = sb.tile([P, PACK, S], F32, name="relus", tag="raw2_0")
+        relus = sb.tile([P, PACK, S], F32, name="relus", tag="raw2_0", align_bytes=64)
         for t in range(PACK):
             y = bank(t, "y%d" % t)
             product(y[:], w1_codes[:, t * P : (t + 1) * P], w1_plane[:, t * P : (t + 1) * P], x_codes[:], x_plane[:])
             nc.scalar.activation(relus[:, t, :], y[:], ACT.Relu)
 
         scaled = sb.tile([P, PACK, V], F32, name="scaled")
-        ments = [sb.tile([P, V], F32, name="ment%d" % t) for t in range(PACK)]
-
-        def gate(gated, t, b):
-            nc.scalar.activation(
-                gated[:, t, :], ments[t][:].indirect(cor_t[:, b * P // 16 : (b + 1) * P // 16]), ACT.Sigmoid
-            )
-
-        gated0 = sb.tile([P, PACK, P], F32, name="gated0")
-
-        def difference(t):
-            yw = bank(4 + t, "yw%d" % t)
+        gated = sb.tile([P, PACK, V], F32, name="gated")
+        for t in range(PACK):
+            yw = bank(PACK + t, "yw%d" % t)
             product(yw[:], w2_codes[:, t * P : (t + 1) * P], w2_plane[:, t * P : (t + 1) * P], x_codes[:], x_plane[:])
-            yr = sb.tile([P, S], F32, name="yr%d" % t, tag="yr%d" % t, align_bytes=64)
-            nc.vector.scalar_tensor_tensor(yr[:], yw[:], -0.5, relus[:, t, :], ALU.mult, ALU.add)
-            return yr
-
-        def mention(t, yr):
-            nc.vector.tensor_tensor(ments[t][:], yr[:, 0:S:2], yr[:, 1:S:2], ALU.max)
-            gate(gated0, t, 0)
-            if t < PACK - 1:
-                nc.scalar.activation(scaled[:, t, :], ments[t][:], ACT.Copy, scale=unit_t[:, t : t + 1])
+            window = sb.tile([P, V + S], F32, name="window%d" % t)
+            nc.vector.scalar_tensor_tensor(window[:, V:], yw[:], -0.5, relus[:, t, :], ALU.mult, ALU.add)
+            nc.vector.tensor_tensor(window[:, :V], window[:, V : V + S : 2], window[:, V + 1 : V + S : 2], ALU.max)
+            nc.scalar.activation(gated[:, t, :], window[:].indirect(cor_t[:]), ACT.Sigmoid)
+            if t == 0:
+                nc.scalar.activation(scaled[:, t, :], window[:, :V], ACT.Copy, scale=unit_t[:, t : t + 1])
             else:
-                nc.vector.tensor_scalar(scaled[:, t, :], ments[t][:], unit_t[:, t : t + 1], None, ALU.mult)
-
-        pending = difference(0)
-        for t in range(PACK):
-            following = difference(t + 1) if t + 1 < PACK else None
-            mention(t, pending)
-            pending = following
-        gated1 = sb.tile([P, PACK, P], F32, name="gated1", tag="yr%d" % (PACK - 1), align_bytes=64)
-        for t in range(PACK):
-            gate(gated1, t, 1)
-        nc.scalar.activation(warm[:, 2:3], gated1[:, PACK - 1, 0:1], ACT.Exp)
+                nc.vector.tensor_scalar(scaled[:, t, :], window[:, :V], unit_t[:, t : t + 1], None, ALU.mult)
+        nc.scalar.activation(warm[:, 2:3], gated[:, PACK - 1, 0:1], ACT.Exp)
 
         def pick_entities(h, tag):
-            codes = sb.tile([P, HALF], U32, name="e_codes%d" % h, tag=tag, align_bytes=64)
-            nc.vector.tensor_copy(codes[:], e_table[:].indirect(ent_t[:, h * HALF // 16 : (h + 1) * HALF // 16]))
+            codes = sb.tile([P, Z_HALF], U32, name="e_codes%d" % h, tag=tag, align_bytes=64)
+            span = Z_HALF // GROUP
+            nc.vector.tensor_copy(codes[:], e_table[:].indirect(ent_t[:, h * span : (h + 1) * span]))
             return codes
 
-        def hidden(b, gated):
+        def hidden(b):
             hid = sb.tile([P, P, PACK], BF16, name="hid%d" % b, tag="hid%d" % b, align_bytes=64)
             nc.vector.tensor_tensor(
                 hid[:].rearrange("p (c i) t -> p c t i", i=4),
                 scaled[:, :, b * P : (b + 1) * P].rearrange("p t (c i) -> p c t i", i=4),
-                gated[:].rearrange("p t (c i) -> p c t i", i=4),
+                gated[:, :, b * P : (b + 1) * P].rearrange("p t (c i) -> p c t i", i=4),
                 ALU.mult,
             )
-            h_codes = sb.tile([P, P], U32, name="h_codes%d" % b, align_bytes=64)
-            h_plane = sb.tile([P, P], U8, name="h_plane%d" % b, align_bytes=64)
+            codes = sb.tile([P, P], U32, name="h_codes%d" % b, align_bytes=64)
+            plane = sb.tile([P, P], U8, name="h_plane%d" % b, align_bytes=64)
             nc.vector.quantize_mx(
-                out=h_codes[:].bitcast(FP8X4), scales=h_plane[:], in_=hid[:].rearrange("p v t -> p (v t)")
+                out=codes[:].bitcast(FP8X4), scales=plane[:], in_=hid[:].rearrange("p v t -> p (v t)")
             )
-            return h_codes, h_plane
+            return codes, plane
 
-        e_codes = [pick_entities(0, "unit")]
-        hidden_mx = [hidden(0, gated0)]
+        e_codes = [pick_entities(0, "raw2_0")]
+        hidden_mx = [hidden(0)]
         e_codes.append(pick_entities(1, "hid0"))
-        hidden_mx.append(hidden(1, gated1))
+        hidden_mx.append(hidden(1))
 
-        for b in range(V // P):
+        for b in range(BLOCKS):
             h_codes, h_plane = hidden_mx[b]
             lp = sb.tile([P, Z], F32, name="lp%d" % b)
             for h in range(2):
-                cols = slice(h * HALF, (h + 1) * HALF)
+                cols = slice(h * Z_HALF, (h + 1) * Z_HALF)
                 sc = bank(2 * b + h, "sc%d_%d" % (b, h))
-                product(sc[:, :HALF], h_codes[:], h_plane[:], e_codes[h][:], e_plane[:, cols])
-                nc.vector.tensor_tensor(lp[:, cols], sc[:, :HALF], log_prior[:, cols], ALU.add)
+                product(sc[:, :Z_HALF], h_codes[:], h_plane[:], e_codes[h][:], e_plane[:, cols])
+                nc.vector.tensor_tensor(lp[:, cols], sc[:, :Z_HALF], log_prior[:, cols], ALU.add)
                 nc.scalar.activation(squashed[b][:, cols], lp[:, cols], ACT.Tanh)
+
             el = sb.tile([P, Z + 1], F32, name="el%d" % b)
             den = sb.tile([P, 1], F32, name="den%d" % b)
             nc.scalar.activation(el[:], squashed[b][:], ACT.Exp, scale=2.0, accum_out=den[:])
@@ -240,11 +237,16 @@ def tile_picked_yentity_nll_p_kernel(
             nc.vector.tensor_tensor_scan(
                 horner[:], ratio[:].to_broadcast([P, TERMS]), series[:], 0.0, ALU.mult, ALU.add
             )
+
             result = sb.tile([P, Z], F32, name="result%d" % b)
             for h in range(2):
-                cols = slice(h * HALF, (h + 1) * HALF)
+                cols = slice(h * Z_HALF, (h + 1) * Z_HALF)
                 nc.vector.tensor_scalar(
-                    result[:, cols], lp[:, cols], horner[:, TERMS - 1 : TERMS], math.log(CENTRE),
-                    ALU.subtract, ALU.subtract,
+                    result[:, cols],
+                    lp[:, cols],
+                    horner[:, TERMS - 1 : TERMS],
+                    math.log(CENTRE),
+                    ALU.subtract,
+                    ALU.subtract,
                 )
                 nc.sync.dma_start(out=out[b * P : (b + 1) * P, cols], in_=result[:, cols])

import math
from contextlib import ExitStack

import concourse.mybir as mybir
from concourse.masks import make_identity

K, T, S, H, V, Z, W = 512, 2048, 512, 512, 256, 512, 2048
FLOPS = 2 * K * H * S * 2 + 2 * H * V * Z

F32 = mybir.dt.float32
BF16 = mybir.dt.bfloat16
I32 = mybir.dt.int32
U32 = mybir.dt.uint32
U16 = mybir.dt.uint16
U8 = mybir.dt.uint8
FP8X4 = mybir.dt.float8_e4m3fn_x4
ALU = mybir.AluOpType
ACT = mybir.ActivationFunctionType

P = 128
PACK = 4
BANK = 512
GROUP = 16
SCALE_ROWS = K // 32
W_HALF = H // 2
Z_HALF = Z // 2
BLOCKS = V // P

TERMS = 64
SHIFT_ARG = 3.25
CENTRE = math.exp(2.0 * SHIFT_ARG) / Z - 0.05


def tile_picked_yentity_nll_p_kernel(
    tc, x_words, x_scales, w1, w2, e_words, e_scales, unit, prior, offs, ent, cor, out
):
    nc = tc.nc
    with ExitStack() as ctx:
        lists = ctx.enter_context(tc.tile_pool(name="lists", bufs=1))
        sb = ctx.enter_context(tc.tile_pool(name="sb", bufs=1))
        psum = ctx.enter_context(tc.psum_pool(name="psum", bufs=1))

        def bank(number, name):
            return psum.tile([P, BANK], F32, name=name, tag="bank%d" % number)

        offs_t = lists.tile([P, S // GROUP], U16, name="offs_t")
        ent_t = lists.tile([P, Z // GROUP], U16, name="ent_t")
        cor_t = lists.tile([P, V // GROUP], U16, name="cor_t")
        x_table = sb.tile([P, T], U32, name="x_table")
        e_table = sb.tile([P, W], U32, name="e_table")
        x_bytes = sb.tile([P, T], U8, name="x_bytes")
        e_bytes = sb.tile([P, W], U8, name="e_bytes")
        prior_t = sb.tile([P, W], F32, name="prior_t")
        unit_t = sb.tile([P, PACK], F32, name="unit_t")
        raw1 = sb.tile([P, PACK, H], F32, name="raw1", tag="raw1")
        raw2 = [
            sb.tile([P, PACK, W_HALF], F32, name="raw2_%d" % h, tag="raw2_%d" % h, align_bytes=64) for h in range(2)
        ]

        def load_scales(table, scales):
            for r in range(4):
                nc.sync.dma_start(out=table[r:P:32, :].bitcast(I32), in_=scales[0, r:SCALE_ROWS:4, :].bitcast(I32))

        def load_words(table, words):
            nc.sync.dma_start(out=table[:].bitcast(I32), in_=words[0].rearrange("p n t -> p (n t)").bitcast(I32))

        squashed = [sb.tile([P, Z + 1], F32, name="squashed%d" % b) for b in range(BLOCKS)]
        for b in range(BLOCKS):
            nc.vector.memset(squashed[b][:, Z:], SHIFT_ARG)
        nc.vector.memset(x_bytes[:].bitcast(I32), 0)
        nc.vector.memset(e_bytes[:].bitcast(I32), 0)
        nc.vector.memset(prior_t[0 : P - 1, :], 0.0)
        warm = sb.tile([P, 3], F32, name="warm")
        nc.scalar.activation(warm[:, 0:1], squashed[0][:, Z:], ACT.Ln)

        nc.sync.dma_start(ent_t[:], ent)
        nc.sync.dma_start(out=prior_t[P - 1 : P, :], in_=prior[0:1, :])
        nc.sync.dma_start(out=raw1[:], in_=w1.rearrange("(p j) c -> p j c", j=PACK))
        nc.sync.dma_start(offs_t[:], offs)
        load_scales(x_bytes, x_scales)
        load_words(x_table, x_words)
        load_scales(e_bytes, e_scales)
        for h in range(2):
            nc.sync.dma_start(
                out=raw2[h][:], in_=w2.rearrange("(p j) c -> p j c", j=PACK)[:, :, h * W_HALF : (h + 1) * W_HALF]
            )
        load_words(e_table, e_words)
        nc.sync.dma_start(cor_t[:], cor)

        ident = sb.tile([P, P], F32, name="ident")
        make_identity(nc, ident[:])

        odd = sb.tile([P, TERMS // 2], F32, name="odd")
        nc.gpsimd.iota(
            odd[:],
            pattern=[[-2, TERMS // 2]],
            base=TERMS - 1,
            channel_multiplier=0,
            allow_small_or_imprecise_dtypes=True,
        )
        half_odd = sb.tile([P, TERMS // 2], F32, name="half_odd")
        nc.gpsimd.tensor_scalar(half_odd[:], odd[:], 0.5, 0.0, ALU.mult, ALU.add)
        series = sb.tile([P, TERMS], F32, name="series")
        nc.gpsimd.memset(series[:], 0.0)

        nc.gpsimd.dma_start(out=unit_t[:], in_=unit.rearrange("(p t) o -> p (t o)", t=PACK))

        prior_picked = sb.tile([P, Z], F32, name="prior_picked")
        nc.scalar.activation(prior_picked[:], prior_t[:].indirect(ent_t[:]), ACT.Copy)
        turned = bank(4, "turned")
        for c in range(Z // P):
            nc.tensor.transpose(turned[:, c * P : (c + 1) * P], prior_picked[:, c * P : (c + 1) * P], ident[:])

        nc.vector.reciprocal(series[:, 0:TERMS:2], half_odd[:])

        def interleave(grouped, halves):
            span = W_HALF // PACK
            for h in range(2):
                dst = grouped[:, :, h * span : (h + 1) * span, :].rearrange("p t m j -> p m t j")
                src = halves[h].rearrange("p j (m t) -> p m t j", t=PACK)
                if h == 0:
                    nc.scalar.copy(dst, src)
                else:
                    nc.vector.tensor_copy(dst, src)

        def quantise(grouped, name):
            codes = sb.tile([P, H], U32, name=name + "_codes", align_bytes=64)
            plane = sb.tile([P, H], U8, name=name + "_plane", align_bytes=64)
            for t in range(PACK):
                nc.vector.quantize_mx(
                    out=codes[:, t * P : (t + 1) * P].bitcast(FP8X4),
                    scales=plane[:, t * P : (t + 1) * P],
                    in_=grouped[:, t, :, :].rearrange("p m j -> p (m j)"),
                )
            return codes, plane

        grouped1 = sb.tile([P, PACK, P, PACK], BF16, name="grouped1", align_bytes=64)
        interleave(grouped1, [raw1[:, :, :W_HALF], raw1[:, :, W_HALF:]])

        log_col = sb.tile([P, Z // P], F32, name="log_col", tag="raw1")
        nc.scalar.activation(log_col[:], turned[:, P - 1 : Z : P], ACT.Ln)
        nc.scalar.activation(warm[:, 1:2], log_col[:, 0:1], ACT.Sigmoid)
        spread = bank(5, "spread")
        for c in range(Z // P):
            nc.tensor.transpose(spread[:, c * P : (c + 1) * P], log_col[:, c : c + 1].to_broadcast([P, P]), ident[:])
        log_prior = sb.tile([P, Z], F32, name="log_prior")
        nc.scalar.copy(log_prior[:], spread[:])

        x_codes = sb.tile([P, S], U32, name="x_codes", align_bytes=64)
        x_plane = sb.tile([P, S], U8, name="x_plane", align_bytes=64)
        e_plane = sb.tile([P, Z], U8, name="e_plane", align_bytes=64)
        nc.vector.tensor_copy(x_plane[:], x_bytes[:].indirect(offs_t[:]))
        w1_codes, w1_plane = quantise(grouped1, "w1")
        nc.vector.tensor_copy(x_codes[:], x_table[:].indirect(offs_t[:]))
        nc.vector.tensor_copy(e_plane[:], e_bytes[:].indirect(ent_t[:]))

        grouped2 = sb.tile([P, PACK, P, PACK], BF16, name="grouped2", align_bytes=64)
        interleave(grouped2, [raw2[0][:], raw2[1][:]])
        w2_codes, w2_plane = quantise(grouped2, "w2")

        def product(acc, lhs_codes, lhs_plane, rhs_codes, rhs_plane):
            nc.tensor.matmul_mx(
                out=acc,
                lhsT=lhs_codes.bitcast(FP8X4),
                lhsT_scale=lhs_plane,
                rhs=rhs_codes.bitcast(FP8X4),
                rhs_scale=rhs_plane,
                start=True,
                stop=True,
            )

        relus = sb.tile([P, PACK, S], F32, name="relus", tag="raw2_0", align_bytes=64)
        for t in range(PACK):
            y = bank(t, "y%d" % t)
            product(y[:], w1_codes[:, t * P : (t + 1) * P], w1_plane[:, t * P : (t + 1) * P], x_codes[:], x_plane[:])
            nc.scalar.activation(relus[:, t, :], y[:], ACT.Relu)

        scaled = sb.tile([P, PACK, V], F32, name="scaled")
        gated = sb.tile([P, PACK, V], F32, name="gated")
        for t in range(PACK):
            yw = bank(PACK + t, "yw%d" % t)
            product(yw[:], w2_codes[:, t * P : (t + 1) * P], w2_plane[:, t * P : (t + 1) * P], x_codes[:], x_plane[:])
            window = sb.tile([P, V + S], F32, name="window%d" % t)
            nc.vector.scalar_tensor_tensor(window[:, V:], yw[:], -0.5, relus[:, t, :], ALU.mult, ALU.add)
            nc.vector.tensor_tensor(window[:, :V], window[:, V : V + S : 2], window[:, V + 1 : V + S : 2], ALU.max)
            nc.scalar.activation(gated[:, t, :], window[:].indirect(cor_t[:]), ACT.Sigmoid)
            if t == 0:
                nc.scalar.activation(scaled[:, t, :], window[:, :V], ACT.Copy, scale=unit_t[:, t : t + 1])
            else:
                nc.vector.tensor_scalar(scaled[:, t, :], window[:, :V], unit_t[:, t : t + 1], None, ALU.mult)
        nc.scalar.activation(warm[:, 2:3], gated[:, PACK - 1, 0:1], ACT.Exp)

        def pick_entities(h, tag):
            codes = sb.tile([P, Z_HALF], U32, name="e_codes%d" % h, tag=tag, align_bytes=64)
            span = Z_HALF // GROUP
            nc.vector.tensor_copy(codes[:], e_table[:].indirect(ent_t[:, h * span : (h + 1) * span]))
            return codes

        def hidden(b):
            hid = sb.tile([P, P, PACK], BF16, name="hid%d" % b, tag="hid%d" % b, align_bytes=64)
            nc.vector.tensor_tensor(
                hid[:].rearrange("p (c i) t -> p c t i", i=4),
                scaled[:, :, b * P : (b + 1) * P].rearrange("p t (c i) -> p c t i", i=4),
                gated[:, :, b * P : (b + 1) * P].rearrange("p t (c i) -> p c t i", i=4),
                ALU.mult,
            )
            codes = sb.tile([P, P], U32, name="h_codes%d" % b, align_bytes=64)
            plane = sb.tile([P, P], U8, name="h_plane%d" % b, align_bytes=64)
            nc.vector.quantize_mx(
                out=codes[:].bitcast(FP8X4), scales=plane[:], in_=hid[:].rearrange("p v t -> p (v t)")
            )
            return codes, plane

        e_codes = [pick_entities(0, "raw2_0")]
        hidden_mx = [hidden(0)]
        e_codes.append(pick_entities(1, "hid0"))
        hidden_mx.append(hidden(1))

        for b in range(BLOCKS):
            h_codes, h_plane = hidden_mx[b]
            lp = sb.tile([P, Z], F32, name="lp%d" % b)
            for h in range(2):
                cols = slice(h * Z_HALF, (h + 1) * Z_HALF)
                sc = bank(2 * b + h, "sc%d_%d" % (b, h))
                product(sc[:, :Z_HALF], h_codes[:], h_plane[:], e_codes[h][:], e_plane[:, cols])
                nc.vector.tensor_tensor(lp[:, cols], sc[:, :Z_HALF], log_prior[:, cols], ALU.add)
                nc.scalar.activation(squashed[b][:, cols], lp[:, cols], ACT.Tanh)

            el = sb.tile([P, Z + 1], F32, name="el%d" % b)
            den = sb.tile([P, 1], F32, name="den%d" % b)
            nc.scalar.activation(el[:], squashed[b][:], ACT.Exp, scale=2.0, accum_out=den[:])
            inv = sb.tile([P, 1], F32, name="inv%d" % b)
            nc.vector.reciprocal(inv[:], den[:])
            ratio = sb.tile([P, 1], F32, name="ratio%d" % b)
            nc.vector.tensor_scalar(ratio[:], inv[:], -2.0 * Z * CENTRE, 1.0, ALU.mult, ALU.add)
            horner = sb.tile([P, TERMS], F32, name="horner%d" % b)
            nc.vector.tensor_tensor_scan(
                horner[:], ratio[:].to_broadcast([P, TERMS]), series[:], 0.0, ALU.mult, ALU.add
            )

            result = sb.tile([P, Z], F32, name="result%d" % b)
            for h in range(2):
                cols = slice(h * Z_HALF, (h + 1) * Z_HALF)
                nc.vector.tensor_scalar(
                    result[:, cols],
                    lp[:, cols],
                    horner[:, TERMS - 1 : TERMS],
                    math.log(CENTRE),
                    ALU.subtract,
                    ALU.subtract,
                )
                nc.sync.dma_start(out=out[b * P : (b + 1) * P, cols], in_=result[:, cols])
